import numpy as np
import ml_dtypes


def mxq(x, axis, fmt="e4m3"):
    dtype, down = {"e4m3": (ml_dtypes.float8_e4m3fn, 7), "e5m2": (ml_dtypes.float8_e5m2, 14)}[fmt]
    v = np.moveaxis(np.asarray(x, np.float32).astype(ml_dtypes.bfloat16).astype(np.float64), axis, -1)
    blocks = v.reshape(v.shape[:-1] + (-1, 32))
    amax = np.abs(blocks).max(-1, keepdims=True)
    byte = np.maximum(np.where(amax > 0, np.frexp(amax)[1] - 1 + 127, 0) - down, 1)
    scale = np.exp2(byte - 127.0)
    codes = (blocks / scale).astype(np.float32).astype(dtype).astype(np.float64)
    return np.moveaxis((codes * scale).reshape(v.shape), -1, axis)


WIDE = False


def mx_kscale(k):
    if not WIDE:
        return np.ones(k)
    levels = np.array([10, -10, 5, -5, 0])
    if k % 512:
        return np.exp2(np.random.permutation(np.resize(levels, k // 32))).repeat(32)
    a = np.empty((k // 512, 16))
    for p in range(k // 512):
        a[p, :8] = np.random.permutation(np.resize(levels, 8))
        for g in range(8):
            far = levels[np.abs(levels - a[p, g]) >= 10]
            a[p, g + 8] = far[np.random.randint(len(far))]
    return np.exp2(a.ravel()).repeat(32)


def f64(x):
    return np.asarray(x).astype(np.float64)


def striped(idx):
    return np.tile(idx.reshape(-1, 16).T, (8, 1)).astype(np.uint16)


def unstriped(offs):
    return offs[:16].T.reshape(-1).astype(np.int64)


E2M1 = np.array([0.0, 0.5, 1.0, 1.5, 2.0, 3.0, 4.0, 6.0, -0.0, -0.5, -1.0, -1.5, -2.0, -3.0, -4.0, -6.0])


def pack_weight(w, fmt):
    k, n = w.shape
    w = f64(np.asarray(w, np.float32).astype(ml_dtypes.bfloat16)).reshape(k // 32, 32, n)
    amax = np.abs(w).max(1)
    if fmt == "e4m3":
        byte = np.frexp(amax)[1] - 1 + 127 - 7
    else:
        mant, ex = np.frexp(amax / 6.0)
        byte = np.where(mant > 0.5, ex, ex - 1) + 127
    byte = np.clip(np.where(amax > 0, byte, 1), 1, 254)
    scaled = (w * np.exp2(127.0 - byte)[:, None, :]).reshape(k, n).astype(np.float32)
    by_word = np.ascontiguousarray(scaled.reshape(k // 512, 128, 4, n).transpose(0, 1, 3, 2))
    if fmt == "e4m3":
        words = by_word.astype(ml_dtypes.float8_e4m3fn).view(np.uint8)
    else:
        c = by_word.astype(ml_dtypes.float4_e2m1fn).view(np.uint8) & 0xF
        words = (c[..., 0::2] | (c[..., 1::2] << 4)).reshape(k // 512, 128, 2 * n)
    return np.ascontiguousarray(words), np.ascontiguousarray(byte.astype(np.uint8).reshape(k // 512, 16, n))


def unpack_weight(words, scales, fmt):
    g, _, n = scales.shape
    words = np.ascontiguousarray(words).reshape(g, 128, n, -1)
    if fmt == "e4m3":
        vals = words.view(ml_dtypes.float8_e4m3fn).astype(np.float64)
    else:
        nib = np.empty((g, 128, n, 4), np.uint8)
        nib[..., 0::2] = words & 0xF
        nib[..., 1::2] = words >> 4
        vals = E2M1[nib]
    vals = vals * np.repeat(np.exp2(scales.astype(np.float64) - 127.0), 8, axis=1)[..., None]
    return vals.transpose(0, 1, 3, 2).reshape(g * 512, n)


def gelu(v):
    return 0.5 * v * (1.0 + np.tanh(np.sqrt(2.0 / np.pi) * (v + 0.044715 * v**3)))


K, T, S, P, H, N = 1024, 4096, 1024, 512, 512, 384


def setup_inputs():
    n = np.random.standard_normal
    s = mx_kscale(K)[:, None]
    u = mx_kscale(H)[:, None]
    d = {}
    d["tab_words"], d["tab_scales"] = pack_weight(n((K, T)) * s, "e2m1")
    d["offs"] = striped(np.random.permutation(T)[:S])
    d["pos1"] = striped(np.random.permutation(S)[:P])
    d["pos2"] = striped(np.random.permutation(S)[:P])
    d["w1"] = (n((K, H)) / s * u.T / K ** 0.5).astype(np.float32)
    d["w2"] = (1.3 * n((K, H)) / s / K ** 0.5).astype(np.float32)
    d["b2"] = (0.7 * n(H)).astype(np.float32)
    d["w3_words"], d["w3_scales"] = pack_weight(n((K, H)) / s * u.T / K ** 0.5, "e4m3")
    d["drift"] = (0.8 * n(H) * u[:, 0]).astype(np.float32)
    d["w4_words"], d["w4_scales"] = pack_weight(n((H, N)) / u / H ** 0.5, "e2m1")
    return d


def reference(tab_words, tab_scales, offs, pos1, pos2, w1, w2, b2, w3_words, w3_scales, drift, w4_words, w4_scales):
    v = unpack_weight(tab_words, tab_scales, "e2m1")[:, unstriped(offs)]
    w3 = unpack_weight(w3_words, w3_scales, "e4m3")
    w4 = unpack_weight(w4_words, w4_scales, "e2m1")
    a = mxq(f64(w1), 0, "e4m3").T @ v
    b = mxq(f64(w2), 0, "e4m3").T @ v
    c = w3.T @ v
    h = a * np.tanh(b + f64(b2)[:, None]) + c
    change = h[:, unstriped(pos1)] - h[:, unstriped(pos2)]
    z = np.abs(change + f64(drift)[:, None])
    return w4.T @ mxq(z, 0, "e4m3")

@@ -1,0 +1,218 @@
+from contextlib import ExitStack
+
+import concourse.mybir as mybir
+
+K, T, S, PAIRS, H, N = 1024, 4096, 1024, 512, 512, 384
+FLOPS = 2 * K * H * S * 3 + 2 * H * N * PAIRS
+
+F32 = mybir.dt.float32
+BF16 = mybir.dt.bfloat16
+I32 = mybir.dt.int32
+U32 = mybir.dt.uint32
+U16 = mybir.dt.uint16
+U8 = mybir.dt.uint8
+FP8X4 = mybir.dt.float8_e4m3fn_x4
+FP4X4 = mybir.dt.float4_e2m1fn_x4
+ACT = mybir.ActivationFunctionType
+ALU = mybir.AluOpType
+
+P = 128
+PACK = 4
+PASSES = K // (P * PACK)
+BANK = 512
+QUADS = 4
+PIECE = 256
+
+
+def tile_list_return_audit_features_kernel(
+    tc, tab_words, tab_scales, offs, pos1, pos2, w1, w2, b2, w3_words, w3_scales, drift, w4_words, w4_scales, out
+):
+    nc = tc.nc
+    with ExitStack() as ctx:
+        keep = ctx.enter_context(tc.tile_pool(name="keep", bufs=1))
+        psum = ctx.enter_context(tc.psum_pool(name="psum", bufs=8))
+
+        def held(name, shape, dtype):
+            return keep.tile(shape, dtype, name=name, align_bytes=64)
+
+        offs_sb = keep.tile([P, S // 16], U16, name="offs_sb")
+        pos1_sb = keep.tile([P, PAIRS // 16], U16, name="pos1_sb")
+        pos2_sb = keep.tile([P, PAIRS // 16], U16, name="pos2_sb")
+
+        tab_sc = held("tab_sc", [P, T], U8)
+        v_sc = [held(f"v_sc{a}", [P, S], U8) for a in range(PASSES)]
+        w3_sc_raw = held("w3_sc_raw", [P, PASSES, H], U8)
+        w4_sc = held("w4_sc", [P, N], U8)
+        nc.vector.memset(tab_sc[0:96, :].bitcast(I32), 0)
+        nc.vector.memset(w3_sc_raw[:].bitcast(I32), 0)
+        for a in range(PASSES):
+            nc.vector.memset(v_sc[a][:].bitcast(I32), 0)
+        nc.vector.memset(w4_sc[:].bitcast(I32), 0)
+
+        nc.sync.dma_start(offs_sb[:], offs)
+        nc.sync.dma_start(tab_sc[96:P, :].bitcast(I32), tab_scales.bitcast(I32).rearrange("a q n -> (a q) n"))
+
+        w3_sc_rows = w3_scales.bitcast(I32).rearrange("a (q r) n -> r q a n", r=4)
+        for r in range(4):
+            nc.gpsimd.dma_start(w3_sc_raw[r:P:32, :, :].bitcast(I32), w3_sc_rows[r])
+        b2_sb = held("b2_sb", [P, PACK], F32)
+        nc.gpsimd.dma_start(b2_sb[:], b2.rearrange("(p t) -> p t", t=PACK))
+
+        def load_weight(name, w, a, c0, c1):
+            raw = held(name, [P, PACK, c1 - c0], F32)
+            rows = w[a * P * PACK : (a + 1) * P * PACK, :].rearrange("(p j) c -> p j c", j=PACK)
+            nc.sync.dma_start(raw[:], rows[:, :, c0:c1])
+            return raw
+
+        def load_table(a):
+            words = held(f"tab_w{a}", [P, T], U16)
+            nc.sync.dma_start(words[:].bitcast(I32), tab_words[a].bitcast(I32))
+            return words
+
+        w2_raw0 = load_weight("w2_raw0", w2, 0, 0, H)
+        tab_w0 = load_table(0)
+        w2_raw1 = load_weight("w2_raw1", w2, 1, 0, H)
+        tab_w1 = load_table(1)
+        w1_raw0 = load_weight("w1_raw0", w1, 0, 0, H)
+        w3_raw = held("w3_raw", [P, PASSES, H], I32)
+        nc.sync.dma_start(w3_raw[:], w3_words.rearrange("a p c i -> p a (c i)").bitcast(I32))
+        w1_raw1 = [load_weight(f"w1_raw1_{u}", w1, 1, u * H // 2, (u + 1) * H // 2) for u in range(2)]
+        nc.sync.dma_start(pos2_sb[:], pos2)
+        nc.sync.dma_start(pos1_sb[:], pos1)
+        drift_sb = held("drift_sb", [P, PACK], F32)
+        nc.sync.dma_start(drift_sb[:], drift.rearrange("(p t) -> p t", t=PACK))
+        w4_w = held("w4_w", [P, 2 * N], U8)
+        nc.sync.dma_start(w4_w[:].bitcast(I32), w4_words[0].bitcast(I32))
+        w4_sc_rows = w4_scales[0].bitcast(I32).rearrange("(q r) n -> r q n", r=4)
+        for r in range(4):
+            nc.sync.dma_start(w4_sc[r:P:32, :].bitcast(I32), w4_sc_rows[r])
+
+        warm = held("warm", [P, 1], F32)
+        nc.scalar.activation(warm[:], b2_sb[:, 0:1], ACT.Tanh)
+
+        v_sc_rows = held("v_sc_rows", [P, S], U8)
+        nc.vector.tensor_copy(v_sc_rows[:], tab_sc[:].indirect(offs_sb[:]))
+        for a in range(PASSES):
+            for q in range(QUADS):
+                row = 96 + 16 * a + 4 * q
+                nc.gpsimd.dma_start(v_sc[a][32 * q : 32 * q + 4, :].bitcast(I32), v_sc_rows[row : row + 4, :].bitcast(I32))
+        v_w = [held(f"v_w{a}", [P, S], U16) for a in range(PASSES)]
+
+        def interleave(copy, grouped, raw, m0, m1):
+            dst = grouped[:].rearrange("p (t m j) -> p m t j", t=PACK, j=PACK)[:, m0:m1]
+            copy(dst, raw[:].rearrange("p j (m t) -> p m t j", t=PACK))
+
+        def quantize(codes, scales, grouped, c0, c1):
+            nc.vector.quantize_mx(
+                out=codes[:, c0:c1].bitcast(FP8X4), scales=scales[:, c0:c1], in_=grouped[:, PACK * c0 : PACK * c1]
+            )
+
+        def weight_tiles(name):
+            return (held(name + "_bf", [P, PACK * H], BF16), held(name + "_q", [P, H], U32), held(name + "_s", [P, H], U8))
+
+        w2_t = [weight_tiles(f"w2_{a}") for a in range(PASSES)]
+        w1_t = [weight_tiles(f"w1_{a}") for a in range(PASSES)]
+
+        interleave(nc.scalar.copy, w2_t[0][0], w2_raw0, 0, P)
+        nc.vector.tensor_copy(v_w[0][:], tab_w0[:].indirect(offs_sb[:]))
+        quantize(w2_t[0][1], w2_t[0][2], w2_t[0][0], 0, H)
+        w3_sc = held("w3_sc", [P, PASSES, H], U8)
+        nc.vector.tensor_copy(
+            w3_sc[:].rearrange("p a (t g i) -> p a g t i", t=PACK, i=16),
+            w3_sc_raw[:].rearrange("p a (g i t) -> p a g t i", t=PACK, i=16),
+        )
+        interleave(nc.scalar.copy, w2_t[1][0], w2_raw1, 0, P)
+        nc.vector.tensor_copy(v_w[1][:], tab_w1[:].indirect(offs_sb[:]))
+        quantize(w2_t[1][1], w2_t[1][2], w2_t[1][0], 0, H)
+        interleave(nc.scalar.copy, w1_t[0][0], w1_raw0, 0, P)
+        w3_q = held("w3_q", [P, PASSES, H], I32)
+        nc.vector.tensor_copy(
+            w3_q[:].rearrange("p a (t g i) -> p a g t i", t=PACK, i=4),
+            w3_raw[:].rearrange("p a (g i t) -> p a g t i", t=PACK, i=4),
+        )
+        for u in range(2):
+            interleave(nc.vector.tensor_copy, w1_t[1][0], w1_raw1[u], u * P // 2, (u + 1) * P // 2)
+        quantize(w1_t[0][1], w1_t[0][2], w1_t[0][0], 0, H)
+        quantize(w1_t[1][1], w1_t[1][2], w1_t[1][0], 0, P)
+        quantize(w1_t[1][1], w1_t[1][2], w1_t[1][0], P, 2 * P)
+        quantize(w1_t[1][1], w1_t[1][2], w1_t[1][0], 2 * P, H)
+
+        def product(codes, scales, t, half):
+            acc = psum.tile([P, BANK], F32, name="acc")
+            rows = slice(t * P, (t + 1) * P)
+            cols = slice(half * BANK, (half + 1) * BANK)
+            for a in range(PASSES):
+                nc.tensor.matmul_mx(
+                    out=acc[:],
+                    lhsT=codes[a][:, rows].bitcast(FP8X4),
+                    lhsT_scale=scales[a][:, rows],
+                    rhs=v_w[a][:, cols].bitcast(FP4X4),
+                    rhs_scale=v_sc[a][:, cols],
+                    start=(a == 0),
+                    stop=(a == PASSES - 1),
+                )
+            return acc
+
+        w1_q, w1_s = [x[1] for x in w1_t], [x[2] for x in w1_t]
+        w2_q, w2_s = [x[1] for x in w2_t], [x[2] for x in w2_t]
+        w3_qs = [w3_q[:, a, :] for a in range(PASSES)]
+        w3_ss = [w3_sc[:, a, :] for a in range(PASSES)]
+
+        z_bf = held("z_bf", [P, PAIRS * PACK], BF16)
+        z_slots = z_bf[:].rearrange("p (j t) -> p t j", t=PACK)
+        halves = range(S // BANK)
+
+        def make_h(t):
+            gate = held(f"gate{t}", [P, S], F32)
+            gated = held(f"gated{t}", [P, S], F32)
+            h = held(f"h{t}", [P, S], F32)
+            for half in halves:
+                b = product(w2_q, w2_s, t, half)
+                nc.scalar.activation(gate[:, half * BANK : (half + 1) * BANK], b[:], ACT.Tanh, bias=b2_sb[:, t : t + 1])
+            for half in halves:
+                cols = slice(half * BANK, (half + 1) * BANK)
+                a_acc = product(w1_q, w1_s, t, half)
+                nc.vector.tensor_tensor(gated[:, cols], a_acc[:], gate[:, cols], ALU.mult)
+            for half in halves:
+                cols = slice(half * BANK, (half + 1) * BANK)
+                c_acc = product(w3_qs, w3_ss, t, half)
+                nc.vector.tensor_tensor(h[:, cols], c_acc[:], gated[:, cols], ALU.add)
+            return h
+
+        def make_z(h, t, j0, j1):
+            last_year = held(f"last_year{t}_{j0}", [P, j1 - j0], F32)
+            change = held(f"change{t}_{j0}", [P, j1 - j0], F32)
+            nc.vector.tensor_copy(last_year[:], h[:].indirect(pos2_sb[:, j0 // 16 : j1 // 16]))
+            nc.vector.tensor_tensor(change[:], h[:].indirect(pos1_sb[:, j0 // 16 : j1 // 16]), last_year[:], ALU.subtract)
+            nc.scalar.activation(z_slots[:, t, j0:j1], change[:], ACT.Abs, bias=drift_sb[:, t : t + 1])
+
+        z_q = held("z_q", [P, PAIRS], U32)
+        z_s = held("z_s", [P, PAIRS], U8)
+        out_rows = out.rearrange("(i p) j -> p i j", p=P)
+
+        def finish(j0, j1, last):
+            quantize(z_q, z_s, z_bf, j0, j1)
+            width = j1 - j0
+            result = held(f"result{j0}", [P, N // P, width], F32)
+            for i in range(N // P):
+                acc = psum.tile([P, BANK], F32, name="acc")
+                nc.tensor.matmul_mx(
+                    out=acc[:, 0:width],
+                    lhsT=w4_w[:, 2 * P * i : 2 * P * (i + 1)].bitcast(FP4X4),
+                    lhsT_scale=w4_sc[:, P * i : P * (i + 1)],
+                    rhs=z_q[:, j0:j1].bitcast(FP8X4),
+                    rhs_scale=z_s[:, j0:j1],
+                    start=True,
+                    stop=True,
+                )
+                copy = nc.vector.tensor_copy if i == 1 or (last and i == 2) else nc.scalar.copy
+                copy(result[:, i, :], acc[:, 0:width])
+            nc.sync.dma_start(out_rows[:, :, j0:j1], result[:])
+
+        for t in range(PACK - 1):
+            make_z(make_h(t), t, 0, PAIRS)
+        h_last = make_h(PACK - 1)
+        for j0 in range(0, PAIRS, PIECE):
+            make_z(h_last, PACK - 1, j0, j0 + PIECE)
+        for j0 in range(0, PAIRS, PIECE):
+            finish(j0, j0 + PIECE, j0 + PIECE == PAIRS)

@@ -21,7 +21,7 @@ PACK = 4
 PASSES = K // (P * PACK)
 BANK = 512
 QUADS = 4
-PIECE = 256
+PIECES = ((0, 256), (256, 384), (384, 512))
 
 
 def tile_list_return_audit_features_kernel(
@@ -32,14 +32,14 @@ def tile_list_return_audit_features_kernel(
         keep = ctx.enter_context(tc.tile_pool(name="keep", bufs=1))
         psum = ctx.enter_context(tc.psum_pool(name="psum", bufs=8))
 
-        def held(name, shape, dtype):
-            return keep.tile(shape, dtype, name=name, align_bytes=64)
+        def held(name, shape, dtype, tag=""):
+            return keep.tile(shape, dtype, name=name, tag=tag, align_bytes=64)
 
         offs_sb = keep.tile([P, S // 16], U16, name="offs_sb")
         pos1_sb = keep.tile([P, PAIRS // 16], U16, name="pos1_sb")
         pos2_sb = keep.tile([P, PAIRS // 16], U16, name="pos2_sb")
 
-        tab_sc = held("tab_sc", [P, T], U8)
+        tab_sc = held("tab_sc", [P, T], U8, "reuse_a")
         v_sc = [held(f"v_sc{a}", [P, S], U8) for a in range(PASSES)]
         w3_sc_raw = held("w3_sc_raw", [P, PASSES, H], U8)
         w4_sc = held("w4_sc", [P, N], U8)
@@ -49,58 +49,61 @@ def tile_list_return_audit_features_kernel(
             nc.vector.memset(v_sc[a][:].bitcast(I32), 0)
         nc.vector.memset(w4_sc[:].bitcast(I32), 0)
 
+        warm_in = held("warm_in", [P, 1], F32)
+        warm = held("warm", [P, 1], F32)
+        nc.gpsimd.memset(warm_in[:], 0.0)
+        nc.scalar.activation(warm[:], warm_in[:], ACT.Tanh)
+
         nc.sync.dma_start(offs_sb[:], offs)
         nc.sync.dma_start(tab_sc[96:P, :].bitcast(I32), tab_scales.bitcast(I32).rearrange("a q n -> (a q) n"))
 
-        w3_sc_rows = w3_scales.bitcast(I32).rearrange("a (q r) n -> r q a n", r=4)
-        for r in range(4):
-            nc.gpsimd.dma_start(w3_sc_raw[r:P:32, :, :].bitcast(I32), w3_sc_rows[r])
-        b2_sb = held("b2_sb", [P, PACK], F32)
-        nc.gpsimd.dma_start(b2_sb[:], b2.rearrange("(p t) -> p t", t=PACK))
-
-        def load_weight(name, w, a, c0, c1):
-            raw = held(name, [P, PACK, c1 - c0], F32)
+        def load_weight(raw, w, a, c0, c1):
             rows = w[a * P * PACK : (a + 1) * P * PACK, :].rearrange("(p j) c -> p j c", j=PACK)
-            nc.sync.dma_start(raw[:], rows[:, :, c0:c1])
-            return raw
+            nc.sync.dma_start(raw, rows[:, :, c0:c1])
 
-        def load_table(a):
-            words = held(f"tab_w{a}", [P, T], U16)
+        def load_table(a, tag):
+            words = held(f"tab_w{a}", [P, T], U16, tag)
             nc.sync.dma_start(words[:].bitcast(I32), tab_words[a].bitcast(I32))
             return words
 
-        w2_raw0 = load_weight("w2_raw0", w2, 0, 0, H)
-        tab_w0 = load_table(0)
-        w2_raw1 = load_weight("w2_raw1", w2, 1, 0, H)
-        tab_w1 = load_table(1)
-        w1_raw0 = load_weight("w1_raw0", w1, 0, 0, H)
-        w3_raw = held("w3_raw", [P, PASSES, H], I32)
-        nc.sync.dma_start(w3_raw[:], w3_words.rearrange("a p c i -> p a (c i)").bitcast(I32))
-        w1_raw1 = [load_weight(f"w1_raw1_{u}", w1, 1, u * H // 2, (u + 1) * H // 2) for u in range(2)]
+        tab_w0 = load_table(0, "reuse_c")
+        b2_sb = held("b2_sb", [P, PACK], F32)
+        nc.sync.dma_start(b2_sb[:], b2.rearrange("(p t) -> p t", t=PACK))
         nc.sync.dma_start(pos2_sb[:], pos2)
         nc.sync.dma_start(pos1_sb[:], pos1)
         drift_sb = held("drift_sb", [P, PACK], F32)
         nc.sync.dma_start(drift_sb[:], drift.rearrange("(p t) -> p t", t=PACK))
         w4_w = held("w4_w", [P, 2 * N], U8)
         nc.sync.dma_start(w4_w[:].bitcast(I32), w4_words[0].bitcast(I32))
+        w2_raw0 = held("w2_raw0", [P, PACK, H], F32, "reuse_b")
+        load_weight(w2_raw0[:], w2, 0, 0, H)
+        tab_w1 = load_table(1, "reuse_d")
+
+        w3_sc_rows = w3_scales.bitcast(I32).rearrange("a (q r) n -> r q a n", r=4)
+        for r in range(4):
+            nc.gpsimd.dma_start(w3_sc_raw[r:P:32, :, :].bitcast(I32), w3_sc_rows[r])
         w4_sc_rows = w4_scales[0].bitcast(I32).rearrange("(q r) n -> r q n", r=4)
         for r in range(4):
-            nc.sync.dma_start(w4_sc[r:P:32, :].bitcast(I32), w4_sc_rows[r])
+            nc.gpsimd.dma_start(w4_sc[r:P:32, :].bitcast(I32), w4_sc_rows[r])
 
-        warm = held("warm", [P, 1], F32)
-        nc.scalar.activation(warm[:], b2_sb[:, 0:1], ACT.Tanh)
 
         v_sc_rows = held("v_sc_rows", [P, S], U8)
         nc.vector.tensor_copy(v_sc_rows[:], tab_sc[:].indirect(offs_sb[:]))
-        for a in range(PASSES):
+
+        def place_scale_rows(a):
             for q in range(QUADS):
                 row = 96 + 16 * a + 4 * q
-                nc.gpsimd.dma_start(v_sc[a][32 * q : 32 * q + 4, :].bitcast(I32), v_sc_rows[row : row + 4, :].bitcast(I32))
+                nc.sync.dma_start(v_sc[a][32 * q : 32 * q + 4, :].bitcast(I32), v_sc_rows[row : row + 4, :].bitcast(I32))
+
+        place_scale_rows(0)
+        w2_raw1 = held("w2_raw1", [P, PACK, H], F32, "reuse_a")
+        load_weight(w2_raw1[:], w2, 1, 0, H)
+        place_scale_rows(1)
         v_w = [held(f"v_w{a}", [P, S], U16) for a in range(PASSES)]
 
         def interleave(copy, grouped, raw, m0, m1):
             dst = grouped[:].rearrange("p (t m j) -> p m t j", t=PACK, j=PACK)[:, m0:m1]
-            copy(dst, raw[:].rearrange("p j (m t) -> p m t j", t=PACK))
+            copy(dst, raw.rearrange("p j (m t) -> p m t j", t=PACK))
 
         def quantize(codes, scales, grouped, c0, c1):
             nc.vector.quantize_mx(
@@ -108,31 +111,41 @@ def tile_list_return_audit_features_kernel(
             )
 
         def weight_tiles(name):
-            return (held(name + "_bf", [P, PACK * H], BF16), held(name + "_q", [P, H], U32), held(name + "_s", [P, H], U8))
+            return (held(name + "_bf", [P, PACK * H], BF16, name + "_bf"), held(name + "_q", [P, H], U32), held(name + "_s", [P, H], U8))
 
         w2_t = [weight_tiles(f"w2_{a}") for a in range(PASSES)]
         w1_t = [weight_tiles(f"w1_{a}") for a in range(PASSES)]
 
-        interleave(nc.scalar.copy, w2_t[0][0], w2_raw0, 0, P)
         nc.vector.tensor_copy(v_w[0][:], tab_w0[:].indirect(offs_sb[:]))
+        w3_raw = held("w3_raw", [P, PASSES, H], I32, "reuse_c")
+        nc.sync.dma_start(w3_raw[:], w3_words.rearrange("a p c i -> p a (c i)").bitcast(I32))
+        interleave(nc.scalar.copy, w2_t[0][0], w2_raw0[:], 0, P)
+        w1_raw0 = held("w1_raw0", [P, PACK, H], F32, "reuse_b")
+        load_weight(w1_raw0[:], w1, 0, 0, H)
+        nc.vector.tensor_copy(v_w[1][:], tab_w1[:].indirect(offs_sb[:]))
+        w1_raw1_row = held("w1_raw1", [P, PACK * H], F32, "reuse_d")
+        w1_raw1 = []
+        for u in range(2):
+            part = w1_raw1_row[:, u * PACK * H // 2 : (u + 1) * PACK * H // 2].rearrange("p (j c) -> p j c", j=PACK)
+            load_weight(part, w1, 1, u * H // 2, (u + 1) * H // 2)
+            w1_raw1.append(part)
         quantize(w2_t[0][1], w2_t[0][2], w2_t[0][0], 0, H)
-        w3_sc = held("w3_sc", [P, PASSES, H], U8)
+        w3_sc = held("w3_sc", [P, PASSES, H], U8, "w2_0_bf")
         nc.vector.tensor_copy(
             w3_sc[:].rearrange("p a (t g i) -> p a g t i", t=PACK, i=16),
             w3_sc_raw[:].rearrange("p a (g i t) -> p a g t i", t=PACK, i=16),
         )
-        interleave(nc.scalar.copy, w2_t[1][0], w2_raw1, 0, P)
-        nc.vector.tensor_copy(v_w[1][:], tab_w1[:].indirect(offs_sb[:]))
-        quantize(w2_t[1][1], w2_t[1][2], w2_t[1][0], 0, H)
-        interleave(nc.scalar.copy, w1_t[0][0], w1_raw0, 0, P)
+        interleave(nc.scalar.copy, w2_t[1][0], w2_raw1[:], 0, P)
         w3_q = held("w3_q", [P, PASSES, H], I32)
         nc.vector.tensor_copy(
             w3_q[:].rearrange("p a (t g i) -> p a g t i", t=PACK, i=4),
             w3_raw[:].rearrange("p a (g i t) -> p a g t i", t=PACK, i=4),
         )
-        for u in range(2):
-            interleave(nc.vector.tensor_copy, w1_t[1][0], w1_raw1[u], u * P // 2, (u + 1) * P // 2)
+        quantize(w2_t[1][1], w2_t[1][2], w2_t[1][0], 0, H)
+        interleave(nc.vector.tensor_copy, w1_t[0][0], w1_raw0[:], 0, P)
+        interleave(nc.scalar.copy, w1_t[1][0], w1_raw1[0], 0, P // 2)
         quantize(w1_t[0][1], w1_t[0][2], w1_t[0][0], 0, H)
+        interleave(nc.vector.tensor_copy, w1_t[1][0], w1_raw1[1], P // 2, P)
         quantize(w1_t[1][1], w1_t[1][2], w1_t[1][0], 0, P)
         quantize(w1_t[1][1], w1_t[1][2], w1_t[1][0], P, 2 * P)
         quantize(w1_t[1][1], w1_t[1][2], w1_t[1][0], 2 * P, H)
@@ -190,29 +203,32 @@ def tile_list_return_audit_features_kernel(
         z_s = held("z_s", [P, PAIRS], U8)
         out_rows = out.rearrange("(i p) j -> p i j", p=P)
 
-        def finish(j0, j1, last):
+        def finish(j0, j1):
             quantize(z_q, z_s, z_bf, j0, j1)
             width = j1 - j0
             result = held(f"result{j0}", [P, N // P, width], F32)
-            for i in range(N // P):
+            per_bank = BANK // width
+            for i0 in range(0, N // P, per_bank):
+                i1 = min(i0 + per_bank, N // P)
                 acc = psum.tile([P, BANK], F32, name="acc")
-                nc.tensor.matmul_mx(
-                    out=acc[:, 0:width],
-                    lhsT=w4_w[:, 2 * P * i : 2 * P * (i + 1)].bitcast(FP4X4),
-                    lhsT_scale=w4_sc[:, P * i : P * (i + 1)],
-                    rhs=z_q[:, j0:j1].bitcast(FP8X4),
-                    rhs_scale=z_s[:, j0:j1],
-                    start=True,
-                    stop=True,
-                )
-                copy = nc.vector.tensor_copy if i == 1 or (last and i == 2) else nc.scalar.copy
-                copy(result[:, i, :], acc[:, 0:width])
+                for i in range(i0, i1):
+                    nc.tensor.matmul_mx(
+                        out=acc[:, (i - i0) * width : (i - i0 + 1) * width],
+                        lhsT=w4_w[:, 2 * P * i : 2 * P * (i + 1)].bitcast(FP4X4),
+                        lhsT_scale=w4_sc[:, P * i : P * (i + 1)],
+                        rhs=z_q[:, j0:j1].bitcast(FP8X4),
+                        rhs_scale=z_s[:, j0:j1],
+                        start=True,
+                        stop=True,
+                    )
+                copy = nc.vector.tensor_copy if j1 == PAIRS else nc.scalar.copy
+                copy(result[:, i0:i1, :].rearrange("p i j -> p (i j)"), acc[:, 0 : (i1 - i0) * width])
             nc.sync.dma_start(out_rows[:, :, j0:j1], result[:])
 
         for t in range(PACK - 1):
             make_z(make_h(t), t, 0, PAIRS)
         h_last = make_h(PACK - 1)
-        for j0 in range(0, PAIRS, PIECE):
-            make_z(h_last, PACK - 1, j0, j0 + PIECE)
-        for j0 in range(0, PAIRS, PIECE):
-            finish(j0, j0 + PIECE, j0 + PIECE == PAIRS)
+        for j0, j1 in PIECES:
+            make_z(h_last, PACK - 1, j0, j1)
+        for j0, j1 in PIECES:
+            finish(j0, j1)

@@ -21,7 +21,12 @@ PACK = 4
 PASSES = K // (P * PACK)
 BANK = 512
 QUADS = 4
-PIECES = ((0, 256), (256, 384), (384, 512))
+QUAD_ROWS = 4
+LIST_ROWS = 16
+SCALE_ROW0 = P - PASSES * QUADS * QUAD_ROWS
+RAW_BYTES = PACK * H * 4
+BANKS = {"acc_b": 4, "acc_a": 2, "acc_c": 2}
+PIECES = ((0, 256), (256, 384), (384, PAIRS))
 
 
 def tile_list_return_audit_features_kernel(
@@ -30,20 +35,21 @@ def tile_list_return_audit_features_kernel(
     nc = tc.nc
     with ExitStack() as ctx:
         keep = ctx.enter_context(tc.tile_pool(name="keep", bufs=1))
-        psum = ctx.enter_context(tc.psum_pool(name="psum", bufs=8))
+        shared = ctx.enter_context(tc.tile_pool(name="shared", bufs=1))
+        psum = ctx.enter_context(tc.psum_pool(name="psum", bufs=1))
 
         def held(name, shape, dtype, tag=""):
             return keep.tile(shape, dtype, name=name, tag=tag, align_bytes=64)
 
-        offs_sb = keep.tile([P, S // 16], U16, name="offs_sb")
-        pos1_sb = keep.tile([P, PAIRS // 16], U16, name="pos1_sb")
-        pos2_sb = keep.tile([P, PAIRS // 16], U16, name="pos2_sb")
+        offs_sb = keep.tile([P, S // LIST_ROWS], U16, name="offs_sb")
+        pos1_sb = keep.tile([P, PAIRS // LIST_ROWS], U16, name="pos1_sb")
+        pos2_sb = keep.tile([P, PAIRS // LIST_ROWS], U16, name="pos2_sb")
 
-        tab_sc = held("tab_sc", [P, T], U8, "reuse_a")
+        tab_sc = shared.tile([P, T], U8, name="tab_sc", offset=RAW_BYTES - T // 2)
         v_sc = [held(f"v_sc{a}", [P, S], U8) for a in range(PASSES)]
         w3_sc_raw = held("w3_sc_raw", [P, PASSES, H], U8)
         w4_sc = held("w4_sc", [P, N], U8)
-        nc.vector.memset(tab_sc[0:96, :].bitcast(I32), 0)
+        nc.vector.memset(tab_sc[0:SCALE_ROW0, :].bitcast(I32), 0)
         nc.vector.memset(w3_sc_raw[:].bitcast(I32), 0)
         for a in range(PASSES):
             nc.vector.memset(v_sc[a][:].bitcast(I32), 0)
@@ -54,11 +60,8 @@ def tile_list_return_audit_features_kernel(
         nc.gpsimd.memset(warm_in[:], 0.0)
         nc.scalar.activation(warm[:], warm_in[:], ACT.Tanh)
 
-        nc.sync.dma_start(offs_sb[:], offs)
-        nc.sync.dma_start(tab_sc[96:P, :].bitcast(I32), tab_scales.bitcast(I32).rearrange("a q n -> (a q) n"))
-
         def load_weight(raw, w, a, c0, c1):
-            rows = w[a * P * PACK : (a + 1) * P * PACK, :].rearrange("(p j) c -> p j c", j=PACK)
+            rows = w[a * P * PACK : (a + 1) * P * PACK, :].rearrange("(p i) c -> p i c", i=PACK)
             nc.sync.dma_start(raw, rows[:, :, c0:c1])
 
         def load_table(a, tag):
@@ -66,7 +69,9 @@ def tile_list_return_audit_features_kernel(
             nc.sync.dma_start(words[:].bitcast(I32), tab_words[a].bitcast(I32))
             return words
 
-        tab_w0 = load_table(0, "reuse_c")
+        nc.sync.dma_start(offs_sb[:], offs)
+        nc.sync.dma_start(tab_sc[SCALE_ROW0:P, :].bitcast(I32), tab_scales.bitcast(I32).rearrange("a g n -> (a g) n"))
+        tab_w0 = load_table(0, "after_tab_w0")
         b2_sb = held("b2_sb", [P, PACK], F32)
         nc.sync.dma_start(b2_sb[:], b2.rearrange("(p t) -> p t", t=PACK))
         nc.sync.dma_start(pos2_sb[:], pos2)
@@ -75,83 +80,87 @@ def tile_list_return_audit_features_kernel(
         nc.sync.dma_start(drift_sb[:], drift.rearrange("(p t) -> p t", t=PACK))
         w4_w = held("w4_w", [P, 2 * N], U8)
         nc.sync.dma_start(w4_w[:].bitcast(I32), w4_words[0].bitcast(I32))
-        w2_raw0 = held("w2_raw0", [P, PACK, H], F32, "reuse_b")
+        w2_raw0 = held("w2_raw0", [P, PACK, H], F32, "after_w2_raw0")
         load_weight(w2_raw0[:], w2, 0, 0, H)
-        tab_w1 = load_table(1, "reuse_d")
+        tab_w1 = load_table(1, "w2_0_q")
 
-        w3_sc_rows = w3_scales.bitcast(I32).rearrange("a (q r) n -> r q a n", r=4)
-        for r in range(4):
-            nc.gpsimd.dma_start(w3_sc_raw[r:P:32, :, :].bitcast(I32), w3_sc_rows[r])
-        w4_sc_rows = w4_scales[0].bitcast(I32).rearrange("(q r) n -> r q n", r=4)
-        for r in range(4):
-            nc.gpsimd.dma_start(w4_sc[r:P:32, :].bitcast(I32), w4_sc_rows[r])
-
+        w3_sc_rows = w3_scales.bitcast(I32).rearrange("a (q s) n -> s q a n", s=QUAD_ROWS)
+        for s in range(QUAD_ROWS):
+            nc.gpsimd.dma_start(w3_sc_raw[s : P : P // QUADS, :, :].bitcast(I32), w3_sc_rows[s])
+        w4_sc_rows = w4_scales[0].bitcast(I32).rearrange("(q s) n -> s q n", s=QUAD_ROWS)
+        for s in range(QUAD_ROWS):
+            nc.gpsimd.dma_start(w4_sc[s : P : P // QUADS, :].bitcast(I32), w4_sc_rows[s])
 
         v_sc_rows = held("v_sc_rows", [P, S], U8)
         nc.vector.tensor_copy(v_sc_rows[:], tab_sc[:].indirect(offs_sb[:]))
 
         def place_scale_rows(a):
             for q in range(QUADS):
-                row = 96 + 16 * a + 4 * q
-                nc.sync.dma_start(v_sc[a][32 * q : 32 * q + 4, :].bitcast(I32), v_sc_rows[row : row + 4, :].bitcast(I32))
+                src = SCALE_ROW0 + (a * QUADS + q) * QUAD_ROWS
+                dst = q * (P // QUADS)
+                nc.sync.dma_start(
+                    v_sc[a][dst : dst + QUAD_ROWS, :].bitcast(I32), v_sc_rows[src : src + QUAD_ROWS, :].bitcast(I32)
+                )
 
         place_scale_rows(0)
-        w2_raw1 = held("w2_raw1", [P, PACK, H], F32, "reuse_a")
+        w2_raw1 = shared.tile([P, PACK, H], F32, name="w2_raw1", offset=0)
         load_weight(w2_raw1[:], w2, 1, 0, H)
+        w1_raw0 = shared.tile([P, PACK, H], F32, name="w1_raw0", offset=RAW_BYTES)
+        load_weight(w1_raw0[:], w1, 0, 0, H)
         place_scale_rows(1)
         v_w = [held(f"v_w{a}", [P, S], U16) for a in range(PASSES)]
 
         def interleave(copy, grouped, raw, m0, m1):
-            dst = grouped[:].rearrange("p (t m j) -> p m t j", t=PACK, j=PACK)[:, m0:m1]
-            copy(dst, raw.rearrange("p j (m t) -> p m t j", t=PACK))
+            dst = grouped[:].rearrange("p (t m i) -> p m t i", t=PACK, i=PACK)[:, m0:m1]
+            copy(dst, raw.rearrange("p i (m t) -> p m t i", t=PACK))
 
         def quantize(codes, scales, grouped, c0, c1):
             nc.vector.quantize_mx(
                 out=codes[:, c0:c1].bitcast(FP8X4), scales=scales[:, c0:c1], in_=grouped[:, PACK * c0 : PACK * c1]
             )
 
-        def weight_tiles(name):
-            return (held(name + "_bf", [P, PACK * H], BF16, name + "_bf"), held(name + "_q", [P, H], U32), held(name + "_s", [P, H], U8))
+        def reorder_columns(dst, src, run):
+            nc.vector.tensor_copy(
+                dst[:].rearrange("p a (t u m) -> p a u t m", t=PACK, m=run),
+                src[:].rearrange("p a (u m t) -> p a u t m", t=PACK, m=run),
+            )
 
-        w2_t = [weight_tiles(f"w2_{a}") for a in range(PASSES)]
-        w1_t = [weight_tiles(f"w1_{a}") for a in range(PASSES)]
+        w2_bf, w2_q, w2_s, w1_bf, w1_q, w1_s = [], [], [], [], [], []
+        for name, grouped, codes, scales in (("w2", w2_bf, w2_q, w2_s), ("w1", w1_bf, w1_q, w1_s)):
+            for a in range(PASSES):
+                grouped.append(held(f"{name}_{a}_bf", [P, PACK * H], BF16, f"{name}_{a}_bf"))
+                codes.append(held(f"{name}_{a}_q", [P, H], U32, f"{name}_{a}_q"))
+                scales.append(held(f"{name}_{a}_s", [P, H], U8))
 
         nc.vector.tensor_copy(v_w[0][:], tab_w0[:].indirect(offs_sb[:]))
-        w3_raw = held("w3_raw", [P, PASSES, H], I32, "reuse_c")
+        w3_raw = held("w3_raw", [P, PASSES, H], I32, "after_tab_w0")
         nc.sync.dma_start(w3_raw[:], w3_words.rearrange("a p c i -> p a (c i)").bitcast(I32))
-        interleave(nc.scalar.copy, w2_t[0][0], w2_raw0[:], 0, P)
-        w1_raw0 = held("w1_raw0", [P, PACK, H], F32, "reuse_b")
-        load_weight(w1_raw0[:], w1, 0, 0, H)
-        nc.vector.tensor_copy(v_w[1][:], tab_w1[:].indirect(offs_sb[:]))
-        w1_raw1_row = held("w1_raw1", [P, PACK * H], F32, "reuse_d")
+        interleave(nc.scalar.copy, w2_bf[0], w2_raw0[:], 0, P)
+        w1_raw1_row = held("w1_raw1", [P, PACK * H], F32, "after_w2_raw0")
         w1_raw1 = []
         for u in range(2):
-            part = w1_raw1_row[:, u * PACK * H // 2 : (u + 1) * PACK * H // 2].rearrange("p (j c) -> p j c", j=PACK)
+            part = w1_raw1_row[:, u * PACK * H // 2 : (u + 1) * PACK * H // 2].rearrange("p (i c) -> p i c", i=PACK)
             load_weight(part, w1, 1, u * H // 2, (u + 1) * H // 2)
             w1_raw1.append(part)
-        quantize(w2_t[0][1], w2_t[0][2], w2_t[0][0], 0, H)
+        nc.vector.tensor_copy(v_w[1][:], tab_w1[:].indirect(offs_sb[:]))
+        quantize(w2_q[0], w2_s[0], w2_bf[0], 0, H)
         w3_sc = held("w3_sc", [P, PASSES, H], U8, "w2_0_bf")
-        nc.vector.tensor_copy(
-            w3_sc[:].rearrange("p a (t g i) -> p a g t i", t=PACK, i=16),
-            w3_sc_raw[:].rearrange("p a (g i t) -> p a g t i", t=PACK, i=16),
-        )
-        interleave(nc.scalar.copy, w2_t[1][0], w2_raw1[:], 0, P)
-        w3_q = held("w3_q", [P, PASSES, H], I32)
-        nc.vector.tensor_copy(
-            w3_q[:].rearrange("p a (t g i) -> p a g t i", t=PACK, i=4),
-            w3_raw[:].rearrange("p a (g i t) -> p a g t i", t=PACK, i=4),
-        )
-        quantize(w2_t[1][1], w2_t[1][2], w2_t[1][0], 0, H)
-        interleave(nc.vector.tensor_copy, w1_t[0][0], w1_raw0[:], 0, P)
-        interleave(nc.scalar.copy, w1_t[1][0], w1_raw1[0], 0, P // 2)
-        quantize(w1_t[0][1], w1_t[0][2], w1_t[0][0], 0, H)
-        interleave(nc.vector.tensor_copy, w1_t[1][0], w1_raw1[1], P // 2, P)
-        quantize(w1_t[1][1], w1_t[1][2], w1_t[1][0], 0, P)
-        quantize(w1_t[1][1], w1_t[1][2], w1_t[1][0], P, 2 * P)
-        quantize(w1_t[1][1], w1_t[1][2], w1_t[1][0], 2 * P, H)
+        reorder_columns(w3_sc, w3_sc_raw, 16)
+        interleave(nc.scalar.copy, w2_bf[1], w2_raw1[:], 0, P)
+        quantize(w2_q[1], w2_s[1], w2_bf[1], 0, H)
+        interleave(nc.scalar.copy, w1_bf[0], w1_raw0[:], 0, P)
+        w3_words_sb = held("w3_words_sb", [P, PASSES, H], I32)
+        reorder_columns(w3_words_sb, w3_raw, 4)
+        interleave(nc.vector.tensor_copy, w1_bf[1], w1_raw1[0], 0, P // 2)
+        quantize(w1_q[0], w1_s[0], w1_bf[0], 0, H)
+        interleave(nc.vector.tensor_copy, w1_bf[1], w1_raw1[1], P // 2, P)
+        for c0, c1 in ((0, P), (P, 2 * P), (2 * P, H)):
+            quantize(w1_q[1], w1_s[1], w1_bf[1], c0, c1)
+        w3_q = [w3_words_sb[:, a, :] for a in range(PASSES)]
+        w3_s = [w3_sc[:, a, :] for a in range(PASSES)]
 
-        def product(codes, scales, t, half):
-            acc = psum.tile([P, BANK], F32, name="acc")
+        def product(role, codes, scales, t, half):
+            acc = psum.tile([P, BANK], F32, name=role, bufs=BANKS[role])
             rows = slice(t * P, (t + 1) * P)
             cols = slice(half * BANK, (half + 1) * BANK)
             for a in range(PASSES):
@@ -166,69 +175,78 @@ def tile_list_return_audit_features_kernel(
                 )
             return acc
 
-        w1_q, w1_s = [x[1] for x in w1_t], [x[2] for x in w1_t]
-        w2_q, w2_s = [x[1] for x in w2_t], [x[2] for x in w2_t]
-        w3_qs = [w3_q[:, a, :] for a in range(PASSES)]
-        w3_ss = [w3_sc[:, a, :] for a in range(PASSES)]
-
         z_bf = held("z_bf", [P, PAIRS * PACK], BF16)
         z_slots = z_bf[:].rearrange("p (j t) -> p t j", t=PACK)
         halves = range(S // BANK)
+        gate = {}
+
+        def make_gates(t):
+            for half in halves:
+                b_acc = product("acc_b", w2_q, w2_s, t, half)
+                gate[t, half] = shared.tile([P, BANK], F32, name="gate", bufs=2, offset=RAW_BYTES)
+                nc.scalar.activation(gate[t, half][:], b_acc[:], ACT.Tanh, bias=b2_sb[:, t : t + 1])
 
         def make_h(t):
-            gate = held(f"gate{t}", [P, S], F32)
             gated = held(f"gated{t}", [P, S], F32)
             h = held(f"h{t}", [P, S], F32)
             for half in halves:
-                b = product(w2_q, w2_s, t, half)
-                nc.scalar.activation(gate[:, half * BANK : (half + 1) * BANK], b[:], ACT.Tanh, bias=b2_sb[:, t : t + 1])
-            for half in halves:
                 cols = slice(half * BANK, (half + 1) * BANK)
-                a_acc = product(w1_q, w1_s, t, half)
-                nc.vector.tensor_tensor(gated[:, cols], a_acc[:], gate[:, cols], ALU.mult)
-            for half in halves:
-                cols = slice(half * BANK, (half + 1) * BANK)
-                c_acc = product(w3_qs, w3_ss, t, half)
-                nc.vector.tensor_tensor(h[:, cols], c_acc[:], gated[:, cols], ALU.add)
+                a_acc = product("acc_a", w1_q, w1_s, t, half)
+                nc.vector.tensor_tensor(gated[:, cols], a_acc[:], gate[t, half][:], ALU.mult)
+                c_acc = product("acc_c", w3_q, w3_s, t, half)
+                if half == 0:
+                    c_sb = held(f"c_sb{t}", [P, BANK], F32)
+                    nc.scalar.copy(c_sb[:], c_acc[:])
+                    nc.gpsimd.tensor_tensor(h[:, cols], gated[:, cols], c_sb[:], ALU.add)
+                else:
+                    nc.vector.tensor_tensor(h[:, cols], c_acc[:], gated[:, cols], ALU.add)
             return h
 
-        def make_z(h, t, j0, j1):
-            last_year = held(f"last_year{t}_{j0}", [P, j1 - j0], F32)
-            change = held(f"change{t}_{j0}", [P, j1 - j0], F32)
-            nc.vector.tensor_copy(last_year[:], h[:].indirect(pos2_sb[:, j0 // 16 : j1 // 16]))
-            nc.vector.tensor_tensor(change[:], h[:].indirect(pos1_sb[:, j0 // 16 : j1 // 16]), last_year[:], ALU.subtract)
-            nc.scalar.activation(z_slots[:, t, j0:j1], change[:], ACT.Abs, bias=drift_sb[:, t : t + 1])
+        def make_z(h, t, pieces):
+            last_year = held(f"last_year{t}", [P, PAIRS], F32)
+            change = held(f"change{t}", [P, PAIRS], F32)
+
+            def pick_last_year(j0, j1):
+                picked = h[:].indirect(pos2_sb[:, j0 // LIST_ROWS : j1 // LIST_ROWS])
+                nc.vector.tensor_copy(last_year[:, j0:j1], picked)
+
+            pick_last_year(*pieces[0])
+            for n, (j0, j1) in enumerate(pieces):
+                if n + 1 < len(pieces):
+                    pick_last_year(*pieces[n + 1])
+                this_year = h[:].indirect(pos1_sb[:, j0 // LIST_ROWS : j1 // LIST_ROWS])
+                nc.vector.tensor_tensor(change[:, j0:j1], this_year, last_year[:, j0:j1], ALU.subtract)
+                nc.scalar.activation(z_slots[:, t, j0:j1], change[:, j0:j1], ACT.Abs, bias=drift_sb[:, t : t + 1])
+
+        make_gates(0)
+        for t in range(PACK):
+            h_slice = make_h(t)
+            if t + 1 < PACK:
+                make_gates(t + 1)
+            make_z(h_slice, t, PIECES if t + 1 == PACK else ((0, PAIRS),))
 
         z_q = held("z_q", [P, PAIRS], U32)
         z_s = held("z_s", [P, PAIRS], U8)
-        out_rows = out.rearrange("(i p) j -> p i j", p=P)
-
-        def finish(j0, j1):
+        out_rows = out.rearrange("(b p) j -> p b j", p=P)
+        blocks = N // P
+        for j0, j1 in PIECES:
             quantize(z_q, z_s, z_bf, j0, j1)
             width = j1 - j0
-            result = held(f"result{j0}", [P, N // P, width], F32)
+            result = held(f"result{j0}", [P, blocks, width], F32)
             per_bank = BANK // width
-            for i0 in range(0, N // P, per_bank):
-                i1 = min(i0 + per_bank, N // P)
-                acc = psum.tile([P, BANK], F32, name="acc")
-                for i in range(i0, i1):
+            for b0 in range(0, blocks, per_bank):
+                b1 = min(b0 + per_bank, blocks)
+                acc = psum.tile([P, BANK], F32, name="acc_b", bufs=BANKS["acc_b"])
+                for b in range(b0, b1):
                     nc.tensor.matmul_mx(
-                        out=acc[:, (i - i0) * width : (i - i0 + 1) * width],
-                        lhsT=w4_w[:, 2 * P * i : 2 * P * (i + 1)].bitcast(FP4X4),
-                        lhsT_scale=w4_sc[:, P * i : P * (i + 1)],
+                        out=acc[:, (b - b0) * width : (b - b0 + 1) * width],
+                        lhsT=w4_w[:, 2 * P * b : 2 * P * (b + 1)].bitcast(FP4X4),
+                        lhsT_scale=w4_sc[:, P * b : P * (b + 1)],
                         rhs=z_q[:, j0:j1].bitcast(FP8X4),
                         rhs_scale=z_s[:, j0:j1],
                         start=True,
                         stop=True,
                     )
                 copy = nc.vector.tensor_copy if j1 == PAIRS else nc.scalar.copy
-                copy(result[:, i0:i1, :].rearrange("p i j -> p (i j)"), acc[:, 0 : (i1 - i0) * width])
+                copy(result[:, b0:b1, :].rearrange("p b j -> p (b j)"), acc[:, 0 : (b1 - b0) * width])
             nc.sync.dma_start(out_rows[:, :, j0:j1], result[:])
-
-        for t in range(PACK - 1):
-            make_z(make_h(t), t, 0, PAIRS)
-        h_last = make_h(PACK - 1)
-        for j0, j1 in PIECES:
-            make_z(h_last, PACK - 1, j0, j1)
-        for j0, j1 in PIECES:
-            finish(j0, j1)

from contextlib import ExitStack

import concourse.mybir as mybir

K, T, S, PAIRS, H, N = 1024, 4096, 1024, 512, 512, 384
FLOPS = 2 * K * H * S * 3 + 2 * H * N * PAIRS

F32 = mybir.dt.float32
BF16 = mybir.dt.bfloat16
I32 = mybir.dt.int32
U32 = mybir.dt.uint32
U16 = mybir.dt.uint16
U8 = mybir.dt.uint8
FP8X4 = mybir.dt.float8_e4m3fn_x4
FP4X4 = mybir.dt.float4_e2m1fn_x4
ACT = mybir.ActivationFunctionType
ALU = mybir.AluOpType

P = 128
PACK = 4
PASSES = K // (P * PACK)
BANK = 512
QUADS = 4
QUAD_ROWS = 4
LIST_ROWS = 16
SCALE_ROW0 = P - PASSES * QUADS * QUAD_ROWS
RAW_BYTES = PACK * H * 4
BANKS = {"acc_b": 4, "acc_a": 2, "acc_c": 2}
PIECES = ((0, 256), (256, 384), (384, PAIRS))


def tile_list_return_audit_features_kernel(
    tc, tab_words, tab_scales, offs, pos1, pos2, w1, w2, b2, w3_words, w3_scales, drift, w4_words, w4_scales, out
):
    nc = tc.nc
    with ExitStack() as ctx:
        keep = ctx.enter_context(tc.tile_pool(name="keep", bufs=1))
        shared = ctx.enter_context(tc.tile_pool(name="shared", bufs=1))
        psum = ctx.enter_context(tc.psum_pool(name="psum", bufs=1))

        def held(name, shape, dtype, tag=""):
            return keep.tile(shape, dtype, name=name, tag=tag, align_bytes=64)

        offs_sb = keep.tile([P, S // LIST_ROWS], U16, name="offs_sb")
        pos1_sb = keep.tile([P, PAIRS // LIST_ROWS], U16, name="pos1_sb")
        pos2_sb = keep.tile([P, PAIRS // LIST_ROWS], U16, name="pos2_sb")

        tab_sc = shared.tile([P, T], U8, name="tab_sc", offset=RAW_BYTES - T // 2)
        v_sc = [held(f"v_sc{a}", [P, S], U8) for a in range(PASSES)]
        w3_sc_raw = held("w3_sc_raw", [P, PASSES, H], U8)
        w4_sc = held("w4_sc", [P, N], U8)
        nc.vector.memset(tab_sc[0:SCALE_ROW0, :].bitcast(I32), 0)
        nc.vector.memset(w3_sc_raw[:].bitcast(I32), 0)
        for a in range(PASSES):
            nc.vector.memset(v_sc[a][:].bitcast(I32), 0)
        nc.vector.memset(w4_sc[:].bitcast(I32), 0)

        warm_in = held("warm_in", [P, 1], F32)
        warm = held("warm", [P, 1], F32)
        nc.gpsimd.memset(warm_in[:], 0.0)
        nc.scalar.activation(warm[:], warm_in[:], ACT.Tanh)

        def load_weight(raw, w, a, c0, c1):
            rows = w[a * P * PACK : (a + 1) * P * PACK, :].rearrange("(p i) c -> p i c", i=PACK)
            nc.sync.dma_start(raw, rows[:, :, c0:c1])

        def load_table(a, tag):
            words = held(f"tab_w{a}", [P, T], U16, tag)
            nc.sync.dma_start(words[:].bitcast(I32), tab_words[a].bitcast(I32))
            return words

        nc.sync.dma_start(offs_sb[:], offs)
        nc.sync.dma_start(tab_sc[SCALE_ROW0:P, :].bitcast(I32), tab_scales.bitcast(I32).rearrange("a g n -> (a g) n"))
        tab_w0 = load_table(0, "after_tab_w0")
        b2_sb = held("b2_sb", [P, PACK], F32)
        nc.sync.dma_start(b2_sb[:], b2.rearrange("(p t) -> p t", t=PACK))
        nc.sync.dma_start(pos2_sb[:], pos2)
        nc.sync.dma_start(pos1_sb[:], pos1)
        drift_sb = held("drift_sb", [P, PACK], F32)
        nc.sync.dma_start(drift_sb[:], drift.rearrange("(p t) -> p t", t=PACK))
        w4_w = held("w4_w", [P, 2 * N], U8)
        nc.sync.dma_start(w4_w[:].bitcast(I32), w4_words[0].bitcast(I32))
        w2_raw0 = held("w2_raw0", [P, PACK, H], F32, "after_w2_raw0")
        load_weight(w2_raw0[:], w2, 0, 0, H)
        tab_w1 = load_table(1, "w2_0_q")

        w3_sc_rows = w3_scales.bitcast(I32).rearrange("a (q s) n -> s q a n", s=QUAD_ROWS)
        for s in range(QUAD_ROWS):
            nc.gpsimd.dma_start(w3_sc_raw[s : P : P // QUADS, :, :].bitcast(I32), w3_sc_rows[s])
        w4_sc_rows = w4_scales[0].bitcast(I32).rearrange("(q s) n -> s q n", s=QUAD_ROWS)
        for s in range(QUAD_ROWS):
            nc.gpsimd.dma_start(w4_sc[s : P : P // QUADS, :].bitcast(I32), w4_sc_rows[s])

        v_sc_rows = held("v_sc_rows", [P, S], U8)
        nc.vector.tensor_copy(v_sc_rows[:], tab_sc[:].indirect(offs_sb[:]))

        def place_scale_rows(a):
            for q in range(QUADS):
                src = SCALE_ROW0 + (a * QUADS + q) * QUAD_ROWS
                dst = q * (P // QUADS)
                nc.sync.dma_start(
                    v_sc[a][dst : dst + QUAD_ROWS, :].bitcast(I32), v_sc_rows[src : src + QUAD_ROWS, :].bitcast(I32)
                )

        place_scale_rows(0)
        w2_raw1 = shared.tile([P, PACK, H], F32, name="w2_raw1", offset=0)
        load_weight(w2_raw1[:], w2, 1, 0, H)
        w1_raw0 = shared.tile([P, PACK, H], F32, name="w1_raw0", offset=RAW_BYTES)
        load_weight(w1_raw0[:], w1, 0, 0, H)
        place_scale_rows(1)
        v_w = [held(f"v_w{a}", [P, S], U16) for a in range(PASSES)]

        def interleave(copy, grouped, raw, m0, m1):
            dst = grouped[:].rearrange("p (t m i) -> p m t i", t=PACK, i=PACK)[:, m0:m1]
            copy(dst, raw.rearrange("p i (m t) -> p m t i", t=PACK))

        def quantize(codes, scales, grouped, c0, c1):
            nc.vector.quantize_mx(
                out=codes[:, c0:c1].bitcast(FP8X4), scales=scales[:, c0:c1], in_=grouped[:, PACK * c0 : PACK * c1]
            )

        def reorder_columns(dst, src, run):
            nc.vector.tensor_copy(
                dst[:].rearrange("p a (t u m) -> p a u t m", t=PACK, m=run),
                src[:].rearrange("p a (u m t) -> p a u t m", t=PACK, m=run),
            )

        w2_bf, w2_q, w2_s, w1_bf, w1_q, w1_s = [], [], [], [], [], []
        for name, grouped, codes, scales in (("w2", w2_bf, w2_q, w2_s), ("w1", w1_bf, w1_q, w1_s)):
            for a in range(PASSES):
                grouped.append(held(f"{name}_{a}_bf", [P, PACK * H], BF16, f"{name}_{a}_bf"))
                codes.append(held(f"{name}_{a}_q", [P, H], U32, f"{name}_{a}_q"))
                scales.append(held(f"{name}_{a}_s", [P, H], U8))

        nc.vector.tensor_copy(v_w[0][:], tab_w0[:].indirect(offs_sb[:]))
        w3_raw = held("w3_raw", [P, PASSES, H], I32, "after_tab_w0")
        nc.sync.dma_start(w3_raw[:], w3_words.rearrange("a p c i -> p a (c i)").bitcast(I32))
        interleave(nc.scalar.copy, w2_bf[0], w2_raw0[:], 0, P)
        w1_raw1_row = held("w1_raw1", [P, PACK * H], F32, "after_w2_raw0")
        w1_raw1 = []
        for u in range(2):
            part = w1_raw1_row[:, u * PACK * H // 2 : (u + 1) * PACK * H // 2].rearrange("p (i c) -> p i c", i=PACK)
            load_weight(part, w1, 1, u * H // 2, (u + 1) * H // 2)
            w1_raw1.append(part)
        nc.vector.tensor_copy(v_w[1][:], tab_w1[:].indirect(offs_sb[:]))
        quantize(w2_q[0], w2_s[0], w2_bf[0], 0, H)
        w3_sc = held("w3_sc", [P, PASSES, H], U8, "w2_0_bf")
        reorder_columns(w3_sc, w3_sc_raw, 16)
        interleave(nc.scalar.copy, w2_bf[1], w2_raw1[:], 0, P)
        quantize(w2_q[1], w2_s[1], w2_bf[1], 0, H)
        interleave(nc.scalar.copy, w1_bf[0], w1_raw0[:], 0, P)
        w3_words_sb = held("w3_words_sb", [P, PASSES, H], I32)
        reorder_columns(w3_words_sb, w3_raw, 4)
        interleave(nc.vector.tensor_copy, w1_bf[1], w1_raw1[0], 0, P // 2)
        quantize(w1_q[0], w1_s[0], w1_bf[0], 0, H)
        interleave(nc.vector.tensor_copy, w1_bf[1], w1_raw1[1], P // 2, P)
        for c0, c1 in ((0, P), (P, 2 * P), (2 * P, H)):
            quantize(w1_q[1], w1_s[1], w1_bf[1], c0, c1)
        w3_q = [w3_words_sb[:, a, :] for a in range(PASSES)]
        w3_s = [w3_sc[:, a, :] for a in range(PASSES)]

        def product(role, codes, scales, t, half):
            acc = psum.tile([P, BANK], F32, name=role, bufs=BANKS[role])
            rows = slice(t * P, (t + 1) * P)
            cols = slice(half * BANK, (half + 1) * BANK)
            for a in range(PASSES):
                nc.tensor.matmul_mx(
                    out=acc[:],
                    lhsT=codes[a][:, rows].bitcast(FP8X4),
                    lhsT_scale=scales[a][:, rows],
                    rhs=v_w[a][:, cols].bitcast(FP4X4),
                    rhs_scale=v_sc[a][:, cols],
                    start=(a == 0),
                    stop=(a == PASSES - 1),
                )
            return acc

        z_bf = held("z_bf", [P, PAIRS * PACK], BF16)
        z_slots = z_bf[:].rearrange("p (j t) -> p t j", t=PACK)
        halves = range(S // BANK)
        gate = {}

        def make_gates(t):
            for half in halves:
                b_acc = product("acc_b", w2_q, w2_s, t, half)
                gate[t, half] = shared.tile([P, BANK], F32, name="gate", bufs=2, offset=RAW_BYTES)
                nc.scalar.activation(gate[t, half][:], b_acc[:], ACT.Tanh, bias=b2_sb[:, t : t + 1])

        def make_h(t):
            gated = held(f"gated{t}", [P, S], F32)
            h = held(f"h{t}", [P, S], F32)
            for half in halves:
                cols = slice(half * BANK, (half + 1) * BANK)
                a_acc = product("acc_a", w1_q, w1_s, t, half)
                nc.vector.tensor_tensor(gated[:, cols], a_acc[:], gate[t, half][:], ALU.mult)
                c_acc = product("acc_c", w3_q, w3_s, t, half)
                if half == 0:
                    c_sb = held(f"c_sb{t}", [P, BANK], F32)
                    nc.scalar.copy(c_sb[:], c_acc[:])
                    nc.gpsimd.tensor_tensor(h[:, cols], gated[:, cols], c_sb[:], ALU.add)
                else:
                    nc.vector.tensor_tensor(h[:, cols], c_acc[:], gated[:, cols], ALU.add)
            return h

        def make_z(h, t, pieces):
            last_year = held(f"last_year{t}", [P, PAIRS], F32)
            change = held(f"change{t}", [P, PAIRS], F32)

            def pick_last_year(j0, j1):
                picked = h[:].indirect(pos2_sb[:, j0 // LIST_ROWS : j1 // LIST_ROWS])
                nc.vector.tensor_copy(last_year[:, j0:j1], picked)

            pick_last_year(*pieces[0])
            for n, (j0, j1) in enumerate(pieces):
                if n + 1 < len(pieces):
                    pick_last_year(*pieces[n + 1])
                this_year = h[:].indirect(pos1_sb[:, j0 // LIST_ROWS : j1 // LIST_ROWS])
                nc.vector.tensor_tensor(change[:, j0:j1], this_year, last_year[:, j0:j1], ALU.subtract)
                nc.scalar.activation(z_slots[:, t, j0:j1], change[:, j0:j1], ACT.Abs, bias=drift_sb[:, t : t + 1])

        make_gates(0)
        for t in range(PACK):
            h_slice = make_h(t)
            if t + 1 < PACK:
                make_gates(t + 1)
            make_z(h_slice, t, PIECES if t + 1 == PACK else ((0, PAIRS),))

        z_q = held("z_q", [P, PAIRS], U32)
        z_s = held("z_s", [P, PAIRS], U8)
        out_rows = out.rearrange("(b p) j -> p b j", p=P)
        blocks = N // P
        for j0, j1 in PIECES:
            quantize(z_q, z_s, z_bf, j0, j1)
            width = j1 - j0
            result = held(f"result{j0}", [P, blocks, width], F32)
            per_bank = BANK // width
            for b0 in range(0, blocks, per_bank):
                b1 = min(b0 + per_bank, blocks)
                acc = psum.tile([P, BANK], F32, name="acc_b", bufs=BANKS["acc_b"])
                for b in range(b0, b1):
                    nc.tensor.matmul_mx(
                        out=acc[:, (b - b0) * width : (b - b0 + 1) * width],
                        lhsT=w4_w[:, 2 * P * b : 2 * P * (b + 1)].bitcast(FP4X4),
                        lhsT_scale=w4_sc[:, P * b : P * (b + 1)],
                        rhs=z_q[:, j0:j1].bitcast(FP8X4),
                        rhs_scale=z_s[:, j0:j1],
                        start=True,
                        stop=True,
                    )
                copy = nc.vector.tensor_copy if j1 == PAIRS else nc.scalar.copy
                copy(result[:, b0:b1, :].rearrange("p b j -> p (b j)"), acc[:, 0 : (b1 - b0) * width])
            nc.sync.dma_start(out_rows[:, :, j0:j1], result[:])
